import numpy as np
import ml_dtypes


def mxq(x, axis, fmt="e4m3"):
    dtype, down = {"e4m3": (ml_dtypes.float8_e4m3fn, 7), "e5m2": (ml_dtypes.float8_e5m2, 14)}[fmt]
    v = np.moveaxis(np.asarray(x, np.float32).astype(ml_dtypes.bfloat16).astype(np.float64), axis, -1)
    blocks = v.reshape(v.shape[:-1] + (-1, 32))
    amax = np.abs(blocks).max(-1, keepdims=True)
    byte = np.maximum(np.where(amax > 0, np.frexp(amax)[1] - 1 + 127, 0) - down, 1)
    scale = np.exp2(byte - 127.0)
    codes = (blocks / scale).astype(np.float32).astype(dtype).astype(np.float64)
    return np.moveaxis((codes * scale).reshape(v.shape), -1, axis)


WIDE = False


def mx_kscale(k):
    if not WIDE:
        return np.ones(k)
    levels = np.array([30, -30])
    if k % 512:
        return np.exp2(np.random.permutation(np.resize(levels, k // 32))).repeat(32)
    a = np.empty((k // 512, 16))
    for p in range(k // 512):
        a[p, :8] = np.random.permutation(np.resize(levels, 8))
        for g in range(8):
            far = levels[np.abs(levels - a[p, g]) >= 10]
            a[p, g + 8] = far[np.random.randint(len(far))]
    return np.exp2(a.ravel()).repeat(32)


BF16 = ml_dtypes.bfloat16


def bf(x):
    return np.asarray(x, np.float32).astype(BF16)


def f64(x):
    return np.asarray(x).astype(np.float64)


E2M1 = np.array([0.0, 0.5, 1.0, 1.5, 2.0, 3.0, 4.0, 6.0, -0.0, -0.5, -1.0, -1.5, -2.0, -3.0, -4.0, -6.0])


def pack_weight(w, fmt):
    k, n = w.shape
    w = f64(bf(w)).reshape(k // 32, 32, n)
    amax = np.abs(w).max(1)
    if fmt == "e4m3":
        byte = np.frexp(amax)[1] - 1 + 127 - 7
    else:
        mant, ex = np.frexp(amax / 6.0)
        byte = np.where(mant > 0.5, ex, ex - 1) + 127
    byte = np.clip(np.where(amax > 0, byte, 1), 1, 254)
    scaled = (w * np.exp2(127.0 - byte)[:, None, :]).reshape(k, n).astype(np.float32)
    by_word = np.ascontiguousarray(scaled.reshape(k // 512, 128, 4, n).transpose(0, 1, 3, 2))
    if fmt == "e4m3":
        words = by_word.astype(ml_dtypes.float8_e4m3fn).view(np.uint8)
    else:
        c = by_word.astype(ml_dtypes.float4_e2m1fn).view(np.uint8) & 0xF
        words = c[..., 0::2] | (c[..., 1::2] << 4)
    return np.ascontiguousarray(words), np.ascontiguousarray(byte.astype(np.uint8).reshape(k // 512, 16, n))


def unpack_weight(words, scales, fmt):
    g, p, n, _ = words.shape
    if fmt == "e4m3":
        vals = np.ascontiguousarray(words).view(ml_dtypes.float8_e4m3fn).astype(np.float64)
    else:
        nib = np.empty((g, p, n, 4), np.uint8)
        nib[..., 0::2] = words & 0xF
        nib[..., 1::2] = words >> 4
        vals = E2M1[nib]
    vals = vals * np.repeat(np.exp2(scales.astype(np.float64) - 127.0), 8, axis=1)[..., None]
    return vals.transpose(0, 1, 3, 2).reshape(g * 512, n)
def pack4(w):
    words, scales = pack_weight(w, "e2m1")
    return words.reshape(words.shape[0], 128, -1), scales


def unpack4(words, scales):
    return unpack_weight(words.reshape(words.shape[0], 128, -1, 2), scales, "e2m1")


M, K, N, C = 2048, 512, 2048, 512

THRESHOLD = 0.8


def setup_inputs():
    s = mx_kscale(K)
    t = mx_kscale(N)
    u = np.random.standard_normal((M, K)) * s
    v = np.random.standard_normal((K, N)) / np.sqrt(K) / s[:, None] * t
    v_words, v_scales = pack4(v)
    d = np.random.laplace(size=(M, N)) * t
    lam = THRESHOLD * (1 + 0.1 * np.random.standard_normal(N)) * t
    f = np.random.standard_normal((N, C)) / np.sqrt(N) / t[:, None]
    return {"u": bf(u),
            "v_words": v_words,
            "v_scales": v_scales,
            "d": bf(d),
            "lam": bf(lam),
            "f": bf(f)}


def reference(u, v_words, v_scales, d, lam, f):
    low = mxq(f64(u), 1, "e4m3") @ unpack4(v_words, v_scales)
    lm = f64(lam)
    r = f64(d) - low
    e = r - np.minimum(np.maximum(r, -lm), lm)
    return mxq(e, 1, "e5m2") @ mxq(f64(f), 0, "e4m3")

@@ -1,0 +1,368 @@
+from contextlib import ExitStack
+
+import concourse.mybir as mybir
+from concourse.masks import make_identity
+
+M, K, N, C = 2048, 512, 2048, 512
+FLOPS = 2 * M * K * N + 2 * M * N * C
+
+F32 = mybir.dt.float32
+BF16 = mybir.dt.bfloat16
+I32 = mybir.dt.int32
+U32 = mybir.dt.uint32
+U8 = mybir.dt.uint8
+E4M3 = mybir.dt.float8_e4m3fn_x4
+E5M2 = mybir.dt.float8_e5m2_x4
+E2M1 = mybir.dt.float4_e2m1fn_x4
+ALU = mybir.AluOpType
+ACT = mybir.ActivationFunctionType
+
+P = 128
+PACK = 4
+W = 512
+TILES = 4
+STRIPS = M // W
+GROUPS = N // W
+UNITS = STRIPS * GROUPS
+
+
+def tile_robust_pca_sparse_step_s9_kernel(tc, u, v_words, v_scales, d, lam, f, out):
+    nc = tc.nc
+    with ExitStack() as ctx:
+        sb = ctx.enter_context(tc.tile_pool(name="sb", bufs=1))
+        ps = ctx.enter_context(tc.psum_pool(name="ps", bufs=1))
+        ctx.enter_context(tc.manual_schedule())
+
+        def sbuf(name, shape, dtype, bufs=1):
+            return sb.tile(shape, dtype, name=name, tag=name, bufs=bufs, align_bytes=64)
+
+        def bank(name, shape):
+            return ps.tile(shape, F32, name=name, tag=name, bufs={"low": 2, "res": 4, "acc": 2}[name])
+
+        u_rows = u.rearrange("(s p j) k -> s p j k", p=P, j=TILES)
+        d_rows = d.rearrange("(s p j) n -> s p j n", p=P, j=TILES)
+        out_rows = out.rearrange("(s p j) c -> s p j c", p=P, j=TILES)
+        f_rows = f.rearrange("(g q t r) c -> g r q t c", q=16, t=PACK, r=8)
+
+        u_raw, d_raw, f_raw = {}, {}, {}
+
+        def load_u(s, h):
+            u_raw[s, h] = sbuf("u_raw", [P, 2, K], BF16, bufs=2 * STRIPS)
+            nc.sync.dma_start(out=u_raw[s, h][:], in_=u_rows[s, :, 2 * h : 2 * h + 2, :])
+
+        def load_d(unit):
+            s, g = divmod(unit, GROUPS)
+            d_raw[unit] = sbuf("d_raw", [P, TILES, W], BF16, bufs=UNITS)
+            nc.sync.dma_start(out=d_raw[unit][:], in_=d_rows[s, :, :, g * W : (g + 1) * W])
+
+        def load_f(g):
+            f_raw[g] = sbuf("f_raw", [P, PACK, C], BF16, bufs=GROUPS)
+            for r in range(8):
+                nc.sync.dma_start(out=f_raw[g][r:P:8, :, :], in_=f_rows[g, r])
+
+        v_plane = sbuf("v_plane", [P, N], U8)
+        nc.vector.memset(v_plane[:].bitcast(I32), 0)
+        ident = sbuf("ident", [P, P], F32)
+        make_identity(nc, ident[:])
+        lam_f32 = sbuf("lam_f32", [P, W], F32)
+        nc.gpsimd.memset(lam_f32[:], 0.0)
+
+        v_first = sbuf("v_first", [P, 2 * W], U8)
+        v_rest = sbuf("v_rest", [P, 2 * (N - W)], U8)
+        lam_rows = sbuf("lam_rows", [P, W], BF16)
+
+        load_u(0, 0)
+        nc.sync.dma_start(out=v_first[:].bitcast(I32), in_=v_words[0][:, 0 : 2 * W].bitcast(I32))
+        for quad in range(4):
+            nc.scalar.dma_start(
+                out=v_plane[32 * quad : 32 * quad + 4, :].bitcast(I32),
+                in_=v_scales[0][4 * quad : 4 * quad + 4, :].bitcast(I32),
+            )
+        load_d(0)
+        load_u(0, 1)
+        nc.scalar.dma_start(out=lam_rows[0:GROUPS, :], in_=lam.rearrange("(g n) -> g n", g=GROUPS))
+        nc.sync.dma_start(out=v_rest[:].bitcast(I32), in_=v_words[0][:, 2 * W : 2 * N].bitcast(I32))
+        load_d(1)
+        load_f(0)
+        load_d(2)
+        load_f(1)
+        load_u(1, 0)
+        load_u(1, 1)
+        load_d(3)
+        load_f(2)
+        load_d(4)
+        load_f(3)
+        for unit in range(5, UNITS):
+            if unit % GROUPS == 1 and unit // GROUPS + 1 < STRIPS:
+                load_u(unit // GROUPS + 1, 0)
+                load_u(unit // GROUPS + 1, 1)
+            load_d(unit)
+
+        def v_cols(g):
+            if g == 0:
+                return v_first[:].bitcast(E2M1)
+            return v_rest[:, 2 * W * (g - 1) : 2 * W * g].bitcast(E2M1)
+
+        u_turned, u_words, u_codes, u_scale = {}, {}, {}, {}
+
+        def turn_u(s, h):
+            u_turned[s, h] = bank("acc", [P, 2, 2, P])
+            for jj in range(2):
+                words = u_raw[s, h][:, jj, :].bitcast(F32)
+                for w in range(2):
+                    nc.tensor.transpose(u_turned[s, h][:, jj, w, :], words[:, w : K // 2 : 2], ident[:])
+
+        def copy_u(s, h, copy):
+            if h == 0:
+                u_words[s] = sbuf("u_words", [P, PACK * W], BF16, bufs=2)
+            half = u_words[s][:, h * 1024 : (h + 1) * 1024].bitcast(F32)
+            copy(
+                out=half.rearrange("p (j m w) -> p j m w", j=2, w=2),
+                in_=u_turned[s, h][:].rearrange("p j w m -> p j m w"),
+            )
+
+        def quant_u(s, lo, hi):
+            if lo == 0:
+                u_codes[s] = sbuf("u_codes", [P, W], U32, bufs=STRIPS)
+                u_scale[s] = sbuf("u_scale", [P, W], U8, bufs=STRIPS)
+            nc.vector.quantize_mx(
+                out=u_codes[s][:, lo:hi].bitcast(E4M3),
+                scales=u_scale[s][:, lo:hi],
+                in_=u_words[s][:, PACK * lo : PACK * hi],
+            )
+
+        f_words, f_codes, f_scale = {}, {}, {}
+
+        def weave(engine, dst, src):
+            o = dst.rearrange("p (c t) -> p c t", t=PACK)
+            i = src.rearrange("p t c -> p c t")
+            if engine == "pool":
+                nc.gpsimd.tensor_scalar(o, i, 1.0, 0.0, ALU.mult, ALU.add)
+            elif engine == "act":
+                nc.scalar.copy(out=o, in_=i)
+            else:
+                nc.vector.tensor_copy(out=o, in_=i)
+
+        def weave_f(g, engine):
+            f_words[g] = sbuf("f_words", [P, PACK * C], BF16, bufs=GROUPS)
+            weave(engine, f_words[g][:], f_raw[g][:])
+
+        def quant_f(g):
+            f_codes[g] = sbuf("f_codes", [P, C], U32, bufs=GROUPS)
+            f_scale[g] = sbuf("f_scale", [P, C], U8, bufs=GROUPS)
+            nc.vector.quantize_mx(out=f_codes[g][:].bitcast(E4M3), scales=f_scale[g][:], in_=f_words[g][:])
+
+        low, resid, turned, upper, sparse, woven, e_codes, e_scale, acc = {}, {}, {}, {}, {}, {}, {}, {}, {}
+
+        def mm_low(unit, j):
+            s, g = divmod(unit, GROUPS)
+            low[unit, j] = bank("low", [P, W])
+            cols = slice(j * P, (j + 1) * P)
+            nc.tensor.matmul_mx(
+                out=low[unit, j][:],
+                lhsT=u_codes[s][:, cols].bitcast(E4M3),
+                lhsT_scale=u_scale[s][:, cols],
+                rhs=v_cols(g),
+                rhs_scale=v_plane[:, g * W : (g + 1) * W],
+                start=True,
+                stop=True,
+            )
+
+        def residual(unit, j):
+            resid[unit, j] = sbuf("resid", [P, W], F32, bufs=2 * TILES)
+            nc.vector.tensor_tensor(
+                out=resid[unit, j][:].rearrange("p (t q r) -> p q t r", t=PACK, r=8),
+                in0=d_raw[unit][:, j, :].rearrange("p (q t r) -> p q t r", t=PACK, r=8),
+                in1=low[unit, j][:].rearrange("p (q t r) -> p q t r", t=PACK, r=8),
+                op=ALU.subtract,
+            )
+
+        def turn_r(unit, t):
+            turned[unit, t] = bank("res", [P, W])
+            for j in range(TILES):
+                nc.tensor.transpose(
+                    turned[unit, t][:, j * P : (j + 1) * P], resid[unit, j][:, t * P : (t + 1) * P], ident[:]
+                )
+
+        def above(unit, t):
+            g = unit % GROUPS
+            upper[unit, t] = sbuf("upper", [P, W], BF16, bufs=2 * PACK)
+            nc.scalar.activation(
+                out=upper[unit, t][:], in_=turned[unit, t][:], func=ACT.Relu, bias=lam_neg[:, t, g : g + 1], scale=1.0
+            )
+
+        def threshold(unit, t):
+            g = unit % GROUPS
+            if t == 0:
+                sparse[unit] = sbuf("sparse", [P, PACK, W], BF16, bufs=2)
+            nc.vector.scalar_tensor_tensor(
+                out=sparse[unit][:, t, :],
+                in0=turned[unit, t][:],
+                scalar=lam_pos[:, t, g : g + 1],
+                in1=upper[unit, t][:],
+                op0=ALU.add,
+                op1=ALU.min,
+            )
+
+        def weave_e(unit, engine, lo, hi):
+            if unit not in woven:
+                woven[unit] = sbuf("woven", [P, PACK * W], BF16, bufs=2)
+            weave(engine, woven[unit][:, PACK * lo : PACK * hi], sparse[unit][:, :, lo:hi])
+
+        def quant_e(unit, lo, hi):
+            if unit not in e_codes:
+                e_codes[unit] = sbuf("e_codes", [P, W], U32, bufs=2 * GROUPS)
+                e_scale[unit] = sbuf("e_scale", [P, W], U8, bufs=2 * GROUPS)
+            nc.vector.quantize_mx(
+                out=e_codes[unit][:, lo:hi].bitcast(E5M2),
+                scales=e_scale[unit][:, lo:hi],
+                in_=woven[unit][:, PACK * lo : PACK * hi],
+            )
+
+        def mm_out(s, j, g, name="acc"):
+            if g == 0:
+                acc[s, j] = bank(name, [P, C])
+            unit = s * GROUPS + g
+            cols = slice(j * P, (j + 1) * P)
+            nc.tensor.matmul_mx(
+                out=acc[s, j][:],
+                lhsT=e_codes[unit][:, cols].bitcast(E5M2),
+                lhsT_scale=e_scale[unit][:, cols],
+                rhs=f_codes[g][:].bitcast(E4M3),
+                rhs_scale=f_scale[g][:],
+                start=(g == 0),
+                stop=(g == GROUPS - 1),
+            )
+
+        def store(s, j, copy):
+            result = sbuf("result", [P, C], F32, bufs=4)
+            copy(out=result[:], in_=acc[s, j][:])
+            nc.sync.dma_start(out=out_rows[s, :, j, :], in_=result[:])
+
+        turn_u(0, 0)
+        copy_u(0, 0, nc.vector.tensor_copy)
+        turn_u(0, 1)
+        copy_u(0, 1, nc.scalar.copy)
+        quant_u(0, 0, W // 2)
+        mm_low(0, 0)
+        mm_low(0, 1)
+        quant_u(0, W // 2, W)
+        nc.vector.tensor_copy(
+            out=lam_f32[0:GROUPS, :].rearrange("g (t q r) -> g q t r", t=PACK, r=8),
+            in_=lam_rows[0:GROUPS, :].rearrange("g (q t r) -> g q t r", t=PACK, r=8),
+        )
+        lam_turned = bank("acc", [P, PACK, P])
+        lam_pos = sbuf("lam_pos", [P, PACK, GROUPS], F32)
+        lam_neg = sbuf("lam_neg", [P, PACK, GROUPS], F32)
+        residual(0, 0)
+        mm_low(0, 2)
+        residual(0, 1)
+        mm_low(0, 3)
+        for t in range(PACK):
+            nc.tensor.transpose(lam_turned[:, t, :], lam_f32[:, t * P : (t + 1) * P], ident[:])
+        nc.scalar.activation(out=lam_neg[:], in_=lam_turned[:, :, 0:GROUPS], func=ACT.Copy, scale=-1.0)
+        nc.scalar.copy(out=lam_pos[:], in_=lam_turned[:, :, 0:GROUPS])
+        residual(0, 2)
+        mm_low(1, 0)
+        residual(0, 3)
+        mm_low(1, 1)
+        weave_f(0, "pool")
+        weave_f(1, "pool")
+        turn_r(0, 0)
+        turn_r(0, 1)
+        above(0, 0)
+        above(0, 1)
+        residual(1, 0)
+        residual(1, 1)
+        mm_low(1, 2)
+        mm_low(1, 3)
+        turn_r(0, 2)
+        turn_r(0, 3)
+        above(0, 2)
+        above(0, 3)
+        residual(1, 2)
+        residual(1, 3)
+        mm_low(2, 0)
+        mm_low(2, 1)
+
+        last = UNITS - 1
+        for unit in range(UNITS):
+            s, g = divmod(unit, GROUPS)
+            nxt, far = unit + 1, unit + 2
+            new_u = g == 0 and s + 1 < STRIPS
+            threshold(unit, 0)
+            threshold(unit, 1)
+            if nxt <= last:
+                turn_r(nxt, 0)
+                turn_r(nxt, 1)
+            if new_u:
+                turn_u(s + 1, 0)
+            if nxt <= last:
+                above(nxt, 0)
+                above(nxt, 1)
+            if new_u:
+                copy_u(s + 1, 0, nc.scalar.copy)
+            if unit in (1, 2):
+                weave_f(unit + 1, "act")
+            if far <= last:
+                residual(far, 0)
+                residual(far, 1)
+                mm_low(far, 2)
+                mm_low(far, 3)
+            if s > 0:
+                mm_out(s - 1, g, 0)
+                mm_out(s - 1, g, 1)
+            if unit == last:
+                mm_out(s - 1, g, 2)
+                mm_out(s - 1, g, 3)
+                weave_e(unit - 1, "act", 3 * P, W)
+                store(s - 1, g, nc.scalar.copy)
+                for j in range(TILES):
+                    mm_out(s, j, 0, "low" if j < 2 else "acc")
+                    mm_out(s, j, 1)
+            threshold(unit, 2)
+            if 0 < unit < last:
+                quant_e(unit - 1, 0, W)
+            if g == 1 and s + 1 < STRIPS:
+                quant_u(s + 1, 0, W)
+            for gf in {1: [0], 2: [1, 2], 3: [3]}.get(unit, []):
+                quant_f(gf)
+            threshold(unit, 3)
+            if unit < last - 1:
+                weave_e(unit, "pool", 0, W)
+            elif unit == last - 1:
+                weave_e(unit, "pool", 0, 3 * P)
+            if nxt <= last:
+                turn_r(nxt, 2)
+                turn_r(nxt, 3)
+            if new_u:
+                turn_u(s + 1, 1)
+            if nxt <= last:
+                above(nxt, 2)
+                above(nxt, 3)
+            if new_u:
+                copy_u(s + 1, 1, nc.scalar.copy)
+            if far <= last:
+                residual(far, 2)
+                residual(far, 3)
+            if far + 1 <= last:
+                mm_low(far + 1, 0)
+                mm_low(far + 1, 1)
+            if s > 0 and unit < last:
+                mm_out(s - 1, g, 2)
+                mm_out(s - 1, g, 3)
+                store(s - 1, g, nc.scalar.copy)
+
+        s = STRIPS - 1
+        weave_e(last, "act", 0, P)
+        weave_e(last, "act", P, 2 * P)
+        quant_e(last - 1, 0, W)
+        for j in range(TILES):
+            mm_out(s, j, 2)
+        weave_e(last, "dve", 2 * P, 3 * P)
+        weave_e(last, "dve", 3 * P, W)
+        for j in (0, 2, 1, 3):
+            quant_e(last, j * P, (j + 1) * P)
+            mm_out(s, j, 3)
+        for j in (0, 2, 1, 3):
+            store(s, j, nc.scalar.copy if j < 2 else nc.vector.tensor_copy)

@@ -24,6 +24,7 @@ TILES = 4
 STRIPS = M // W
 GROUPS = N // W
 UNITS = STRIPS * GROUPS
+SCALAR_COLS = 128
 
 
 def tile_robust_pca_sparse_step_s9_kernel(tc, u, v_words, v_scales, d, lam, f, out):
@@ -46,14 +47,18 @@ def tile_robust_pca_sparse_step_s9_kernel(tc, u, v_words, v_scales, d, lam, f, o
 
         u_raw, d_raw, f_raw = {}, {}, {}
 
-        def load_u(s, h):
-            u_raw[s, h] = sbuf("u_raw", [P, 2, K], BF16, bufs=2 * STRIPS)
-            nc.sync.dma_start(out=u_raw[s, h][:], in_=u_rows[s, :, 2 * h : 2 * h + 2, :])
+        def load_u(s, lo, hi):
+            piece = sbuf("u_raw", [P, hi - lo, K], BF16, bufs=2 * STRIPS + 1)
+            nc.sync.dma_start(out=piece[:], in_=u_rows[s, :, lo:hi, :])
+            for j in range(lo, hi):
+                u_raw[s, j] = piece[:, j - lo, :]
 
-        def load_d(unit):
+        def load_d(unit, lo, hi):
             s, g = divmod(unit, GROUPS)
-            d_raw[unit] = sbuf("d_raw", [P, TILES, W], BF16, bufs=UNITS)
-            nc.sync.dma_start(out=d_raw[unit][:], in_=d_rows[s, :, :, g * W : (g + 1) * W])
+            piece = sbuf("d_raw%d" % (hi - lo), [P, hi - lo, W], BF16, bufs=UNITS - 1 if hi - lo == TILES else 2)
+            nc.sync.dma_start(out=piece[:], in_=d_rows[s, :, lo:hi, g * W : (g + 1) * W])
+            for j in range(lo, hi):
+                d_raw[unit, j] = piece[:, j - lo, :]
 
         def load_f(g):
             f_raw[g] = sbuf("f_raw", [P, PACK, C], BF16, bufs=GROUPS)
@@ -67,58 +72,62 @@ def tile_robust_pca_sparse_step_s9_kernel(tc, u, v_words, v_scales, d, lam, f, o
         lam_f32 = sbuf("lam_f32", [P, W], F32)
         nc.gpsimd.memset(lam_f32[:], 0.0)
 
-        v_first = sbuf("v_first", [P, 2 * W], U8)
-        v_rest = sbuf("v_rest", [P, 2 * (N - W)], U8)
         lam_rows = sbuf("lam_rows", [P, W], BF16)
+        v_codes = {}
 
-        load_u(0, 0)
-        nc.sync.dma_start(out=v_first[:].bitcast(I32), in_=v_words[0][:, 0 : 2 * W].bitcast(I32))
+        def load_v(g):
+            v_codes[g] = sbuf("v_codes", [P, 2 * W], U8, bufs=GROUPS)
+            nc.sync.dma_start(
+                out=v_codes[g][:].bitcast(I32), in_=v_words[0][:, 2 * W * g : 2 * W * (g + 1)].bitcast(I32)
+            )
+
+        nc.scalar.dma_start(out=lam_rows[0:GROUPS, :], in_=lam.rearrange("(g n) -> g n", g=GROUPS))
+        load_u(0, 0, 1)
+        load_v(0)
         for quad in range(4):
-            nc.scalar.dma_start(
+            nc.sync.dma_start(
                 out=v_plane[32 * quad : 32 * quad + 4, :].bitcast(I32),
                 in_=v_scales[0][4 * quad : 4 * quad + 4, :].bitcast(I32),
             )
-        load_d(0)
-        load_u(0, 1)
-        nc.scalar.dma_start(out=lam_rows[0:GROUPS, :], in_=lam.rearrange("(g n) -> g n", g=GROUPS))
-        nc.sync.dma_start(out=v_rest[:].bitcast(I32), in_=v_words[0][:, 2 * W : 2 * N].bitcast(I32))
-        load_d(1)
+        load_u(0, 1, 2)
+        load_d(0, 0, 2)
+        load_u(0, 2, 4)
+        load_d(0, 2, 4)
+        load_v(1)
+        load_d(1, 0, TILES)
+        load_v(2)
         load_f(0)
-        load_d(2)
+        load_d(2, 0, TILES)
+        load_u(1, 0, 2)
         load_f(1)
-        load_u(1, 0)
-        load_u(1, 1)
-        load_d(3)
+        load_u(1, 2, 4)
+        load_v(3)
+        load_d(3, 0, TILES)
         load_f(2)
-        load_d(4)
+        load_d(4, 0, TILES)
         load_f(3)
         for unit in range(5, UNITS):
             if unit % GROUPS == 1 and unit // GROUPS + 1 < STRIPS:
-                load_u(unit // GROUPS + 1, 0)
-                load_u(unit // GROUPS + 1, 1)
-            load_d(unit)
-
-        def v_cols(g):
-            if g == 0:
-                return v_first[:].bitcast(E2M1)
-            return v_rest[:, 2 * W * (g - 1) : 2 * W * g].bitcast(E2M1)
+                load_u(unit // GROUPS + 1, 0, 2)
+                load_u(unit // GROUPS + 1, 2, 4)
+            load_d(unit, 0, TILES)
 
         u_turned, u_words, u_codes, u_scale = {}, {}, {}, {}
 
-        def turn_u(s, h):
-            u_turned[s, h] = bank("acc", [P, 2, 2, P])
-            for jj in range(2):
-                words = u_raw[s, h][:, jj, :].bitcast(F32)
+        def turn_u(s, lo, hi):
+            u_turned[s, lo] = bank("acc", [P, hi - lo, 2, P])
+            for j in range(lo, hi):
+                words = u_raw[s, j].bitcast(F32)
                 for w in range(2):
-                    nc.tensor.transpose(u_turned[s, h][:, jj, w, :], words[:, w : K // 2 : 2], ident[:])
+                    nc.tensor.transpose(u_turned[s, lo][:, j - lo, w, :], words[:, w : K // 2 : 2], ident[:])
 
-        def copy_u(s, h, copy):
-            if h == 0:
+        def copy_u(s, lo, hi):
+            if lo == 0:
                 u_words[s] = sbuf("u_words", [P, PACK * W], BF16, bufs=2)
-            half = u_words[s][:, h * 1024 : (h + 1) * 1024].bitcast(F32)
-            copy(
-                out=half.rearrange("p (j m w) -> p j m w", j=2, w=2),
-                in_=u_turned[s, h][:].rearrange("p j w m -> p j m w"),
+            part = u_words[s][:, lo * PACK * P : hi * PACK * P].bitcast(F32)
+            nc.scalar.copy(
+                out=part.rearrange("p (j m w) -> p j m w", m=P, w=2),
+                in_=u_turned[s, lo][:].rearrange("p j w m -> p j m w"),
             )
 
         def quant_u(s, lo, hi):
@@ -152,6 +161,7 @@ def tile_robust_pca_sparse_step_s9_kernel(tc, u, v_words, v_scales, d, lam, f, o
             f_scale[g] = sbuf("f_scale", [P, C], U8, bufs=GROUPS)
             nc.vector.quantize_mx(out=f_codes[g][:].bitcast(E4M3), scales=f_scale[g][:], in_=f_words[g][:])
 
+        lower = {}
         low, resid, turned, upper, sparse, woven, e_codes, e_scale, acc = {}, {}, {}, {}, {}, {}, {}, {}, {}
 
         def mm_low(unit, j):
@@ -162,7 +172,7 @@ def tile_robust_pca_sparse_step_s9_kernel(tc, u, v_words, v_scales, d, lam, f, o
                 out=low[unit, j][:],
                 lhsT=u_codes[s][:, cols].bitcast(E4M3),
                 lhsT_scale=u_scale[s][:, cols],
-                rhs=v_cols(g),
+                rhs=v_codes[g][:].bitcast(E2M1),
                 rhs_scale=v_plane[:, g * W : (g + 1) * W],
                 start=True,
                 stop=True,
@@ -172,7 +182,7 @@ def tile_robust_pca_sparse_step_s9_kernel(tc, u, v_words, v_scales, d, lam, f, o
             resid[unit, j] = sbuf("resid", [P, W], F32, bufs=2 * TILES)
             nc.vector.tensor_tensor(
                 out=resid[unit, j][:].rearrange("p (t q r) -> p q t r", t=PACK, r=8),
-                in0=d_raw[unit][:, j, :].rearrange("p (q t r) -> p q t r", t=PACK, r=8),
+                in0=d_raw[unit, j].rearrange("p (q t r) -> p q t r", t=PACK, r=8),
                 in1=low[unit, j][:].rearrange("p (q t r) -> p q t r", t=PACK, r=8),
                 op=ALU.subtract,
             )
@@ -184,30 +194,52 @@ def tile_robust_pca_sparse_step_s9_kernel(tc, u, v_words, v_scales, d, lam, f, o
                     turned[unit, t][:, j * P : (j + 1) * P], resid[unit, j][:, t * P : (t + 1) * P], ident[:]
                 )
 
+        def split(unit):
+            return 0 if unit in (2, 3, UNITS - 1) else SCALAR_COLS
+
         def above(unit, t):
-            g = unit % GROUPS
-            upper[unit, t] = sbuf("upper", [P, W], BF16, bufs=2 * PACK)
-            nc.scalar.activation(
-                out=upper[unit, t][:], in_=turned[unit, t][:], func=ACT.Relu, bias=lam_neg[:, t, g : g + 1], scale=1.0
-            )
+            g, c = unit % GROUPS, split(unit)
+            if t == 0:
+                upper[unit] = sbuf("upper", [P, PACK, W], BF16, bufs=2)
+                if c:
+                    lower[unit] = sbuf("lower", [P, PACK, c], BF16, bufs=2)
+            bias = lam_neg[:, t, g : g + 1]
+            nc.scalar.activation(out=upper[unit][:, t, :], in_=turned[unit, t][:], func=ACT.Relu, bias=bias, scale=1.0)
+            if c:
+                nc.scalar.activation(
+                    out=lower[unit][:, t, :], in_=turned[unit, t][:, 0:c], func=ACT.Relu, bias=bias, scale=-1.0
+                )
 
         def threshold(unit, t):
-            g = unit % GROUPS
+            g, c = unit % GROUPS, split(unit)
             if t == 0:
                 sparse[unit] = sbuf("sparse", [P, PACK, W], BF16, bufs=2)
             nc.vector.scalar_tensor_tensor(
-                out=sparse[unit][:, t, :],
-                in0=turned[unit, t][:],
+                out=sparse[unit][:, t, c:W],
+                in0=turned[unit, t][:, c:W],
                 scalar=lam_pos[:, t, g : g + 1],
-                in1=upper[unit, t][:],
+                in1=upper[unit][:, t, c:W],
                 op0=ALU.add,
                 op1=ALU.min,
             )
 
-        def weave_e(unit, engine, lo, hi):
+        def woven_cols(unit, lo, hi):
             if unit not in woven:
-                woven[unit] = sbuf("woven", [P, PACK * W], BF16, bufs=2)
-            weave(engine, woven[unit][:, PACK * lo : PACK * hi], sparse[unit][:, :, lo:hi])
+                woven[unit] = sbuf("woven", [P, PACK * W], BF16, bufs=3)
+            return woven[unit][:, PACK * lo : PACK * hi]
+
+        def weave_e(unit, engine, lo, hi):
+            weave(engine, woven_cols(unit, lo, hi), sparse[unit][:, :, lo:hi])
+
+        def weave_diff(unit):
+            c = split(unit)
+            if c:
+                nc.gpsimd.tensor_tensor(
+                    out=woven_cols(unit, 0, c).rearrange("p (c t) -> p c t", t=PACK),
+                    in0=upper[unit][:, :, 0:c].rearrange("p t c -> p c t"),
+                    in1=lower[unit][:].rearrange("p t c -> p c t"),
+                    op=ALU.subtract,
+                )
 
         def quant_e(unit, lo, hi):
             if unit not in e_codes:
@@ -239,29 +271,34 @@ def tile_robust_pca_sparse_step_s9_kernel(tc, u, v_words, v_scales, d, lam, f, o
             copy(out=result[:], in_=acc[s, j][:])
             nc.sync.dma_start(out=out_rows[s, :, j, :], in_=result[:])
 
-        turn_u(0, 0)
-        copy_u(0, 0, nc.vector.tensor_copy)
-        turn_u(0, 1)
-        copy_u(0, 1, nc.scalar.copy)
-        quant_u(0, 0, W // 2)
-        mm_low(0, 0)
-        mm_low(0, 1)
-        quant_u(0, W // 2, W)
-        nc.vector.tensor_copy(
+        nc.scalar.activation(
             out=lam_f32[0:GROUPS, :].rearrange("g (t q r) -> g q t r", t=PACK, r=8),
             in_=lam_rows[0:GROUPS, :].rearrange("g (q t r) -> g q t r", t=PACK, r=8),
+            func=ACT.Copy,
+            scale=-1.0,
         )
+        turn_u(0, 0, 1)
+        copy_u(0, 0, 1)
+        turn_u(0, 1, 2)
+        copy_u(0, 1, 2)
+        quant_u(0, 0, P)
+        mm_low(0, 0)
+        turn_u(0, 2, 4)
+        copy_u(0, 2, 4)
+        quant_u(0, P, 2 * P)
+        mm_low(0, 1)
         lam_turned = bank("acc", [P, PACK, P])
         lam_pos = sbuf("lam_pos", [P, PACK, GROUPS], F32)
         lam_neg = sbuf("lam_neg", [P, PACK, GROUPS], F32)
         residual(0, 0)
+        quant_u(0, 2 * P, W)
         mm_low(0, 2)
         residual(0, 1)
         mm_low(0, 3)
         for t in range(PACK):
             nc.tensor.transpose(lam_turned[:, t, :], lam_f32[:, t * P : (t + 1) * P], ident[:])
-        nc.scalar.activation(out=lam_neg[:], in_=lam_turned[:, :, 0:GROUPS], func=ACT.Copy, scale=-1.0)
-        nc.scalar.copy(out=lam_pos[:], in_=lam_turned[:, :, 0:GROUPS])
+        nc.scalar.copy(out=lam_neg[:], in_=lam_turned[:, :, 0:GROUPS])
+        nc.scalar.activation(out=lam_pos[:], in_=lam_turned[:, :, 0:GROUPS], func=ACT.Copy, scale=-1.0)
         residual(0, 2)
         mm_low(1, 0)
         residual(0, 3)
@@ -280,6 +317,7 @@ def tile_robust_pca_sparse_step_s9_kernel(tc, u, v_words, v_scales, d, lam, f, o
         turn_r(0, 3)
         above(0, 2)
         above(0, 3)
+        weave_diff(0)
         residual(1, 2)
         residual(1, 3)
         mm_low(2, 0)
@@ -296,12 +334,12 @@ def tile_robust_pca_sparse_step_s9_kernel(tc, u, v_words, v_scales, d, lam, f, o
                 turn_r(nxt, 0)
                 turn_r(nxt, 1)
             if new_u:
-                turn_u(s + 1, 0)
+                turn_u(s + 1, 0, 2)
             if nxt <= last:
                 above(nxt, 0)
                 above(nxt, 1)
             if new_u:
-                copy_u(s + 1, 0, nc.scalar.copy)
+                copy_u(s + 1, 0, 2)
             if unit in (1, 2):
                 weave_f(unit + 1, "act")
             if far <= last:
@@ -315,33 +353,31 @@ def tile_robust_pca_sparse_step_s9_kernel(tc, u, v_words, v_scales, d, lam, f, o
             if unit == last:
                 mm_out(s - 1, g, 2)
                 mm_out(s - 1, g, 3)
-                weave_e(unit - 1, "act", 3 * P, W)
                 store(s - 1, g, nc.scalar.copy)
                 for j in range(TILES):
                     mm_out(s, j, 0, "low" if j < 2 else "acc")
                     mm_out(s, j, 1)
             threshold(unit, 2)
-            if 0 < unit < last:
+            threshold(unit, 3)
+            if 0 < unit:
                 quant_e(unit - 1, 0, W)
             if g == 1 and s + 1 < STRIPS:
                 quant_u(s + 1, 0, W)
             for gf in {1: [0], 2: [1, 2], 3: [3]}.get(unit, []):
                 quant_f(gf)
-            threshold(unit, 3)
-            if unit < last - 1:
-                weave_e(unit, "pool", 0, W)
-            elif unit == last - 1:
-                weave_e(unit, "pool", 0, 3 * P)
+            if unit < last:
+                weave_e(unit, "pool", split(unit), W)
             if nxt <= last:
                 turn_r(nxt, 2)
                 turn_r(nxt, 3)
             if new_u:
-                turn_u(s + 1, 1)
+                turn_u(s + 1, 2, 4)
             if nxt <= last:
                 above(nxt, 2)
                 above(nxt, 3)
+                weave_diff(nxt)
             if new_u:
-                copy_u(s + 1, 1, nc.scalar.copy)
+                copy_u(s + 1, 2, 4)
             if far <= last:
                 residual(far, 2)
                 residual(far, 3)
@@ -356,13 +392,14 @@ def tile_robust_pca_sparse_step_s9_kernel(tc, u, v_words, v_scales, d, lam, f, o
         s = STRIPS - 1
         weave_e(last, "act", 0, P)
         weave_e(last, "act", P, 2 * P)
-        quant_e(last - 1, 0, W)
         for j in range(TILES):
             mm_out(s, j, 2)
         weave_e(last, "dve", 2 * P, 3 * P)
+        quant_e(last, 0, P)
+        mm_out(s, 0, 3)
         weave_e(last, "dve", 3 * P, W)
-        for j in (0, 2, 1, 3):
+        for j in (2, 1, 3):
             quant_e(last, j * P, (j + 1) * P)
             mm_out(s, j, 3)
         for j in (0, 2, 1, 3):
-            store(s, j, nc.scalar.copy if j < 2 else nc.vector.tensor_copy)
+            store(s, j, nc.scalar.copy if j % 2 == 0 else nc.vector.tensor_copy)

@@ -24,7 +24,8 @@ TILES = 4
 STRIPS = M // W
 GROUPS = N // W
 UNITS = STRIPS * GROUPS
-SCALAR_COLS = 128
+SCALAR_COLS = 304
+FIRST_COLS = 0
 
 
 def tile_robust_pca_sparse_step_s9_kernel(tc, u, v_words, v_scales, d, lam, f, out):
@@ -48,21 +49,22 @@ def tile_robust_pca_sparse_step_s9_kernel(tc, u, v_words, v_scales, d, lam, f, o
         u_raw, d_raw, f_raw = {}, {}, {}
 
         def load_u(s, lo, hi):
-            piece = sbuf("u_raw", [P, hi - lo, K], BF16, bufs=2 * STRIPS + 1)
+            piece = sbuf("u_raw", [P, hi - lo, K], BF16, bufs=2 * STRIPS)
             nc.sync.dma_start(out=piece[:], in_=u_rows[s, :, lo:hi, :])
             for j in range(lo, hi):
                 u_raw[s, j] = piece[:, j - lo, :]
 
         def load_d(unit, lo, hi):
             s, g = divmod(unit, GROUPS)
-            piece = sbuf("d_raw%d" % (hi - lo), [P, hi - lo, W], BF16, bufs=UNITS - 1 if hi - lo == TILES else 2)
+            piece = sbuf("d_raw", [P, hi - lo, W], BF16, bufs=UNITS)
             nc.sync.dma_start(out=piece[:], in_=d_rows[s, :, lo:hi, g * W : (g + 1) * W])
             for j in range(lo, hi):
                 d_raw[unit, j] = piece[:, j - lo, :]
 
-        def load_f(g):
-            f_raw[g] = sbuf("f_raw", [P, PACK, C], BF16, bufs=GROUPS)
-            for r in range(8):
+        def load_f(g, lo=0, hi=8):
+            if lo == 0:
+                f_raw[g] = sbuf("f_raw", [P, PACK, C], BF16, bufs=GROUPS)
+            for r in range(lo, hi):
                 nc.sync.dma_start(out=f_raw[g][r:P:8, :, :], in_=f_rows[g, r])
 
         v_plane = sbuf("v_plane", [P, N], U8)
@@ -81,27 +83,26 @@ def tile_robust_pca_sparse_step_s9_kernel(tc, u, v_words, v_scales, d, lam, f, o
                 out=v_codes[g][:].bitcast(I32), in_=v_words[0][:, 2 * W * g : 2 * W * (g + 1)].bitcast(I32)
             )
 
-        nc.scalar.dma_start(out=lam_rows[0:GROUPS, :], in_=lam.rearrange("(g n) -> g n", g=GROUPS))
-        load_u(0, 0, 1)
+        load_u(0, 0, 2)
+        load_u(0, 2, 4)
         load_v(0)
         for quad in range(4):
             nc.sync.dma_start(
                 out=v_plane[32 * quad : 32 * quad + 4, :].bitcast(I32),
                 in_=v_scales[0][4 * quad : 4 * quad + 4, :].bitcast(I32),
             )
-        load_u(0, 1, 2)
-        load_d(0, 0, 2)
-        load_u(0, 2, 4)
-        load_d(0, 2, 4)
+        load_d(0, 0, TILES)
+        nc.sync.dma_start(out=lam_rows[0:GROUPS, :], in_=lam.rearrange("(g n) -> g n", g=GROUPS))
         load_v(1)
         load_d(1, 0, TILES)
         load_v(2)
         load_f(0)
+        load_f(1, 0, 4)
         load_d(2, 0, TILES)
+        load_f(1, 4, 8)
         load_u(1, 0, 2)
-        load_f(1)
-        load_u(1, 2, 4)
         load_v(3)
+        load_u(1, 2, 4)
         load_d(3, 0, TILES)
         load_f(2)
         load_d(4, 0, TILES)
@@ -143,18 +144,22 @@ def tile_robust_pca_sparse_step_s9_kernel(tc, u, v_words, v_scales, d, lam, f, o
         f_words, f_codes, f_scale = {}, {}, {}
 
         def weave(engine, dst, src):
-            o = dst.rearrange("p (c t) -> p c t", t=PACK)
-            i = src.rearrange("p t c -> p c t")
             if engine == "pool":
+                o = dst.rearrange("p (c t) -> p c t", t=PACK)
+                i = src.rearrange("p t c -> p c t")
                 nc.gpsimd.tensor_scalar(o, i, 1.0, 0.0, ALU.mult, ALU.add)
-            elif engine == "act":
-                nc.scalar.copy(out=o, in_=i)
             else:
-                nc.vector.tensor_copy(out=o, in_=i)
+                o = dst.rearrange("p (c i t) -> p c t i", i=4, t=PACK)
+                i = src.rearrange("p t (c i) -> p c t i", i=4)
+                if engine == "act":
+                    nc.scalar.copy(out=o, in_=i)
+                else:
+                    nc.vector.tensor_copy(out=o, in_=i)
 
-        def weave_f(g, engine):
-            f_words[g] = sbuf("f_words", [P, PACK * C], BF16, bufs=GROUPS)
-            weave(engine, f_words[g][:], f_raw[g][:])
+        def weave_f(g, engine, lo, hi):
+            if lo == 0:
+                f_words[g] = sbuf("f_words", [P, PACK * C], BF16, bufs=GROUPS)
+            weave(engine, f_words[g][:, PACK * lo : PACK * hi], f_raw[g][:, :, lo:hi])
 
         def quant_f(g):
             f_codes[g] = sbuf("f_codes", [P, C], U32, bufs=GROUPS)
@@ -195,7 +200,7 @@ def tile_robust_pca_sparse_step_s9_kernel(tc, u, v_words, v_scales, d, lam, f, o
                 )
 
         def split(unit):
-            return 0 if unit in (2, 3, UNITS - 1) else SCALAR_COLS
+            return FIRST_COLS if unit == 0 else 0 if unit >= UNITS - 2 else SCALAR_COLS
 
         def above(unit, t):
             g, c = unit % GROUPS, split(unit)
@@ -231,14 +236,11 @@ def tile_robust_pca_sparse_step_s9_kernel(tc, u, v_words, v_scales, d, lam, f, o
         def weave_e(unit, engine, lo, hi):
             weave(engine, woven_cols(unit, lo, hi), sparse[unit][:, :, lo:hi])
 
-        def weave_diff(unit):
+        def difference(unit):
             c = split(unit)
             if c:
-                nc.gpsimd.tensor_tensor(
-                    out=woven_cols(unit, 0, c).rearrange("p (c t) -> p c t", t=PACK),
-                    in0=upper[unit][:, :, 0:c].rearrange("p t c -> p c t"),
-                    in1=lower[unit][:].rearrange("p t c -> p c t"),
-                    op=ALU.subtract,
+                nc.vector.tensor_tensor(
+                    out=sparse[unit][:, :, 0:c], in0=upper[unit][:, :, 0:c], in1=lower[unit][:], op=ALU.subtract
                 )
 
         def quant_e(unit, lo, hi):
@@ -271,40 +273,33 @@ def tile_robust_pca_sparse_step_s9_kernel(tc, u, v_words, v_scales, d, lam, f, o
             copy(out=result[:], in_=acc[s, j][:])
             nc.sync.dma_start(out=out_rows[s, :, j, :], in_=result[:])
 
-        nc.scalar.activation(
+        for j in range(TILES):
+            turn_u(0, j, j + 1)
+            copy_u(0, j, j + 1)
+            quant_u(0, j * P, (j + 1) * P)
+        mm_low(0, 0)
+        mm_low(0, 1)
+        nc.vector.tensor_copy(
             out=lam_f32[0:GROUPS, :].rearrange("g (t q r) -> g q t r", t=PACK, r=8),
             in_=lam_rows[0:GROUPS, :].rearrange("g (q t r) -> g q t r", t=PACK, r=8),
-            func=ACT.Copy,
-            scale=-1.0,
         )
-        turn_u(0, 0, 1)
-        copy_u(0, 0, 1)
-        turn_u(0, 1, 2)
-        copy_u(0, 1, 2)
-        quant_u(0, 0, P)
-        mm_low(0, 0)
-        turn_u(0, 2, 4)
-        copy_u(0, 2, 4)
-        quant_u(0, P, 2 * P)
-        mm_low(0, 1)
-        lam_turned = bank("acc", [P, PACK, P])
-        lam_pos = sbuf("lam_pos", [P, PACK, GROUPS], F32)
-        lam_neg = sbuf("lam_neg", [P, PACK, GROUPS], F32)
         residual(0, 0)
-        quant_u(0, 2 * P, W)
         mm_low(0, 2)
         residual(0, 1)
         mm_low(0, 3)
-        for t in range(PACK):
-            nc.tensor.transpose(lam_turned[:, t, :], lam_f32[:, t * P : (t + 1) * P], ident[:])
-        nc.scalar.copy(out=lam_neg[:], in_=lam_turned[:, :, 0:GROUPS])
-        nc.scalar.activation(out=lam_pos[:], in_=lam_turned[:, :, 0:GROUPS], func=ACT.Copy, scale=-1.0)
         residual(0, 2)
         mm_low(1, 0)
         residual(0, 3)
         mm_low(1, 1)
-        weave_f(0, "pool")
-        weave_f(1, "pool")
+        lam_turned = bank("acc", [P, PACK, P])
+        lam_pos = sbuf("lam_pos", [P, PACK, GROUPS], F32)
+        lam_neg = sbuf("lam_neg", [P, PACK, GROUPS], F32)
+        for t in range(PACK):
+            nc.tensor.transpose(lam_turned[:, t, :], lam_f32[:, t * P : (t + 1) * P], ident[:])
+        nc.scalar.activation(out=lam_neg[:], in_=lam_turned[:, :, 0:GROUPS], func=ACT.Copy, scale=-1.0)
+        nc.scalar.copy(out=lam_pos[:], in_=lam_turned[:, :, 0:GROUPS])
+        weave_f(0, "pool", 0, C)
+        weave_f(1, "pool", 0, C)
         turn_r(0, 0)
         turn_r(0, 1)
         above(0, 0)
@@ -317,7 +312,6 @@ def tile_robust_pca_sparse_step_s9_kernel(tc, u, v_words, v_scales, d, lam, f, o
         turn_r(0, 3)
         above(0, 2)
         above(0, 3)
-        weave_diff(0)
         residual(1, 2)
         residual(1, 3)
         mm_low(2, 0)
@@ -327,67 +321,82 @@ def tile_robust_pca_sparse_step_s9_kernel(tc, u, v_words, v_scales, d, lam, f, o
         for unit in range(UNITS):
             s, g = divmod(unit, GROUPS)
             nxt, far = unit + 1, unit + 2
-            new_u = g == 0 and s + 1 < STRIPS
+            more_u = s + 1 < STRIPS
             threshold(unit, 0)
             threshold(unit, 1)
+            if more_u and g == 1:
+                turn_u(s + 1, 2, 4)
+                copy_u(s + 1, 2, 4)
             if nxt <= last:
                 turn_r(nxt, 0)
                 turn_r(nxt, 1)
-            if new_u:
+            if more_u and g == 0:
                 turn_u(s + 1, 0, 2)
             if nxt <= last:
                 above(nxt, 0)
                 above(nxt, 1)
-            if new_u:
+            if more_u and g == 0:
                 copy_u(s + 1, 0, 2)
-            if unit in (1, 2):
-                weave_f(unit + 1, "act")
             if far <= last:
                 residual(far, 0)
                 residual(far, 1)
                 mm_low(far, 2)
                 mm_low(far, 3)
-            if s > 0:
+            if s > 0 and far <= last:
                 mm_out(s - 1, g, 0)
                 mm_out(s - 1, g, 1)
+            if unit == last - 1:
+                for gg in range(GROUPS):
+                    mm_out(s - 1, 3, gg)
+                store(s - 1, 3, nc.scalar.copy)
+                mm_out(s, 0, 0, "low")
+                mm_out(s, 1, 0, "low")
             if unit == last:
-                mm_out(s - 1, g, 2)
-                mm_out(s - 1, g, 3)
-                store(s - 1, g, nc.scalar.copy)
-                for j in range(TILES):
-                    mm_out(s, j, 0, "low" if j < 2 else "acc")
-                    mm_out(s, j, 1)
+                weave_e(unit - 1, "act", 3 * P, W)
             threshold(unit, 2)
-            threshold(unit, 3)
-            if 0 < unit:
+            if unit == last - 1:
                 quant_e(unit - 1, 0, W)
-            if g == 1 and s + 1 < STRIPS:
+            threshold(unit, 3)
+            if 0 < unit and unit != last - 1:
+                quant_e(unit - 1, 0, W)
+            if more_u and g == 1:
                 quant_u(s + 1, 0, W)
-            for gf in {1: [0], 2: [1, 2], 3: [3]}.get(unit, []):
-                quant_f(gf)
-            if unit < last:
-                weave_e(unit, "pool", split(unit), W)
+            if 1 <= unit <= GROUPS:
+                quant_f(unit - 1)
+            difference(unit)
+            if unit < last - 1:
+                weave_e(unit, "pool", 0, W)
+            elif unit < last:
+                weave_e(unit, "pool", 0, 3 * P)
             if nxt <= last:
                 turn_r(nxt, 2)
                 turn_r(nxt, 3)
-            if new_u:
-                turn_u(s + 1, 2, 4)
             if nxt <= last:
                 above(nxt, 2)
                 above(nxt, 3)
-                weave_diff(nxt)
-            if new_u:
-                copy_u(s + 1, 2, 4)
+            for gf, lo in {1: [(2, 0), (2, C // 2)], 2: [(3, 0)], 3: [(3, C // 2)]}.get(unit, []):
+                weave_f(gf, "act", lo, lo + C // 2)
+            if s > 0 and far <= last:
+                mm_out(s - 1, g, 2)
+                mm_out(s - 1, g, 3)
+            if unit == last - 1:
+                mm_out(s, 0, 1)
+                mm_out(s, 1, 1)
+                for j in (2, 3):
+                    mm_out(s, j, 0)
+                    mm_out(s, j, 1)
             if far <= last:
                 residual(far, 2)
                 residual(far, 3)
             if far + 1 <= last:
                 mm_low(far + 1, 0)
                 mm_low(far + 1, 1)
-            if s > 0 and unit < last:
-                mm_out(s - 1, g, 2)
-                mm_out(s - 1, g, 3)
+            if s > 0 and far <= last:
                 store(s - 1, g, nc.scalar.copy)
+            if far == last:
+                for gg in range(GROUPS):
+                    mm_out(s - 1, 2, gg)
+                store(s - 1, 2, nc.scalar.copy)
 
         s = STRIPS - 1
         weave_e(last, "act", 0, P)

@@ -24,8 +24,9 @@ TILES = 4
 STRIPS = M // W
 GROUPS = N // W
 UNITS = STRIPS * GROUPS
-SCALAR_COLS = 304
+SCALAR_COLS = 288
 FIRST_COLS = 0
+EARLY_COLS = 272
 
 
 def tile_robust_pca_sparse_step_s9_kernel(tc, u, v_words, v_scales, d, lam, f, out):
@@ -54,12 +55,19 @@ def tile_robust_pca_sparse_step_s9_kernel(tc, u, v_words, v_scales, d, lam, f, o
             for j in range(lo, hi):
                 u_raw[s, j] = piece[:, j - lo, :]
 
-        def load_d(unit, lo, hi):
+        def load_d(unit):
             s, g = divmod(unit, GROUPS)
-            piece = sbuf("d_raw", [P, hi - lo, W], BF16, bufs=UNITS)
-            nc.sync.dma_start(out=piece[:], in_=d_rows[s, :, lo:hi, g * W : (g + 1) * W])
-            for j in range(lo, hi):
-                d_raw[unit, j] = piece[:, j - lo, :]
+            piece = sbuf("d_raw", [P, TILES, W], BF16, bufs=UNITS)
+            nc.sync.dma_start(out=piece[:], in_=d_rows[s, :, :, g * W : (g + 1) * W])
+            for j in range(TILES):
+                d_raw[unit, j] = piece[:, j, :]
+
+        def load_d_first(lo):
+            piece = sbuf("d_raw", [P, 2, 2 * W], BF16, bufs=UNITS)
+            nc.sync.dma_start(out=piece[:], in_=d_rows[0, :, lo : lo + 2, 0 : 2 * W])
+            for j in (lo, lo + 1):
+                for g in range(2):
+                    d_raw[g, j] = piece[:, j - lo, g * W : (g + 1) * W]
 
         def load_f(g, lo=0, hi=8):
             if lo == 0:
@@ -78,40 +86,40 @@ def tile_robust_pca_sparse_step_s9_kernel(tc, u, v_words, v_scales, d, lam, f, o
         v_codes = {}
 
         def load_v(g):
-            v_codes[g] = sbuf("v_codes", [P, 2 * W], U8, bufs=GROUPS)
-            nc.sync.dma_start(
-                out=v_codes[g][:].bitcast(I32), in_=v_words[0][:, 2 * W * g : 2 * W * (g + 1)].bitcast(I32)
-            )
+            piece = sbuf("v_codes", [P, 4 * W], U8, bufs=2)
+            nc.sync.dma_start(out=piece[:].bitcast(I32), in_=v_words[0][:, 2 * W * g : 2 * W * (g + 2)].bitcast(I32))
+            v_codes[g] = piece[:, 0 : 2 * W]
+            v_codes[g + 1] = piece[:, 2 * W : 4 * W]
 
         load_u(0, 0, 2)
-        load_u(0, 2, 4)
         load_v(0)
         for quad in range(4):
             nc.sync.dma_start(
                 out=v_plane[32 * quad : 32 * quad + 4, :].bitcast(I32),
                 in_=v_scales[0][4 * quad : 4 * quad + 4, :].bitcast(I32),
             )
-        load_d(0, 0, TILES)
+        load_d_first(0)
+        load_u(0, 2, 4)
+        load_d_first(2)
         nc.sync.dma_start(out=lam_rows[0:GROUPS, :], in_=lam.rearrange("(g n) -> g n", g=GROUPS))
-        load_v(1)
-        load_d(1, 0, TILES)
-        load_v(2)
         load_f(0)
+        load_v(2)
         load_f(1, 0, 4)
-        load_d(2, 0, TILES)
+        load_d(2)
         load_f(1, 4, 8)
         load_u(1, 0, 2)
-        load_v(3)
         load_u(1, 2, 4)
-        load_d(3, 0, TILES)
+        load_d(3)
         load_f(2)
-        load_d(4, 0, TILES)
+        load_u(2, 0, 2)
+        load_d(4)
+        load_u(2, 2, 4)
         load_f(3)
-        for unit in range(5, UNITS):
-            if unit % GROUPS == 1 and unit // GROUPS + 1 < STRIPS:
-                load_u(unit // GROUPS + 1, 0, 2)
-                load_u(unit // GROUPS + 1, 2, 4)
-            load_d(unit, 0, TILES)
+        load_d(5)
+        load_u(3, 0, 2)
+        load_u(3, 2, 4)
+        for unit in range(6, UNITS):
+            load_d(unit)
 
         u_turned, u_words, u_codes, u_scale = {}, {}, {}, {}
 
@@ -177,7 +185,7 @@ def tile_robust_pca_sparse_step_s9_kernel(tc, u, v_words, v_scales, d, lam, f, o
                 out=low[unit, j][:],
                 lhsT=u_codes[s][:, cols].bitcast(E4M3),
                 lhsT_scale=u_scale[s][:, cols],
-                rhs=v_codes[g][:].bitcast(E2M1),
+                rhs=v_codes[g].bitcast(E2M1),
                 rhs_scale=v_plane[:, g * W : (g + 1) * W],
                 start=True,
                 stop=True,
@@ -200,7 +208,7 @@ def tile_robust_pca_sparse_step_s9_kernel(tc, u, v_words, v_scales, d, lam, f, o
                 )
 
         def split(unit):
-            return FIRST_COLS if unit == 0 else 0 if unit >= UNITS - 2 else SCALAR_COLS
+            return FIRST_COLS if unit == 0 else 0 if unit >= UNITS - 2 else EARLY_COLS if 2 <= unit <= 4 else SCALAR_COLS
 
         def above(unit, t):
             g, c = unit % GROUPS, split(unit)
@@ -215,15 +223,16 @@ def tile_robust_pca_sparse_step_s9_kernel(tc, u, v_words, v_scales, d, lam, f, o
                     out=lower[unit][:, t, :], in_=turned[unit, t][:, 0:c], func=ACT.Relu, bias=bias, scale=-1.0
                 )
 
-        def threshold(unit, t):
-            g, c = unit % GROUPS, split(unit)
-            if t == 0:
+        def threshold(unit, t, lo=None, hi=W):
+            g = unit % GROUPS
+            c = split(unit) if lo is None else lo
+            if unit not in sparse:
                 sparse[unit] = sbuf("sparse", [P, PACK, W], BF16, bufs=2)
             nc.vector.scalar_tensor_tensor(
-                out=sparse[unit][:, t, c:W],
-                in0=turned[unit, t][:, c:W],
+                out=sparse[unit][:, t, c:hi],
+                in0=turned[unit, t][:, c:hi],
                 scalar=lam_pos[:, t, g : g + 1],
-                in1=upper[unit][:, t, c:W],
+                in1=upper[unit][:, t, c:hi],
                 op0=ALU.add,
                 op1=ALU.min,
             )
@@ -273,24 +282,31 @@ def tile_robust_pca_sparse_step_s9_kernel(tc, u, v_words, v_scales, d, lam, f, o
             copy(out=result[:], in_=acc[s, j][:])
             nc.sync.dma_start(out=out_rows[s, :, j, :], in_=result[:])
 
-        for j in range(TILES):
+        def first_u(j):
             turn_u(0, j, j + 1)
             copy_u(0, j, j + 1)
-            quant_u(0, j * P, (j + 1) * P)
+
+        first_u(0)
+        first_u(1)
+        quant_u(0, 0, P)
         mm_low(0, 0)
+        mm_low(1, 0)
+        quant_u(0, P, 2 * P)
+        first_u(2)
+        first_u(3)
+        residual(0, 0)
         mm_low(0, 1)
+        residual(1, 0)
+        mm_low(1, 1)
+        quant_u(0, 2 * P, W)
         nc.vector.tensor_copy(
             out=lam_f32[0:GROUPS, :].rearrange("g (t q r) -> g q t r", t=PACK, r=8),
             in_=lam_rows[0:GROUPS, :].rearrange("g (q t r) -> g q t r", t=PACK, r=8),
         )
-        residual(0, 0)
-        mm_low(0, 2)
         residual(0, 1)
+        mm_low(0, 2)
+        residual(1, 1)
         mm_low(0, 3)
-        residual(0, 2)
-        mm_low(1, 0)
-        residual(0, 3)
-        mm_low(1, 1)
         lam_turned = bank("acc", [P, PACK, P])
         lam_pos = sbuf("lam_pos", [P, PACK, GROUPS], F32)
         lam_neg = sbuf("lam_neg", [P, PACK, GROUPS], F32)
@@ -298,117 +314,123 @@ def tile_robust_pca_sparse_step_s9_kernel(tc, u, v_words, v_scales, d, lam, f, o
             nc.tensor.transpose(lam_turned[:, t, :], lam_f32[:, t * P : (t + 1) * P], ident[:])
         nc.scalar.activation(out=lam_neg[:], in_=lam_turned[:, :, 0:GROUPS], func=ACT.Copy, scale=-1.0)
         nc.scalar.copy(out=lam_pos[:], in_=lam_turned[:, :, 0:GROUPS])
+        residual(0, 2)
+        mm_low(1, 2)
+        residual(0, 3)
+        mm_low(1, 3)
         weave_f(0, "pool", 0, C)
         weave_f(1, "pool", 0, C)
-        turn_r(0, 0)
-        turn_r(0, 1)
-        above(0, 0)
-        above(0, 1)
-        residual(1, 0)
-        residual(1, 1)
-        mm_low(1, 2)
-        mm_low(1, 3)
-        turn_r(0, 2)
-        turn_r(0, 3)
-        above(0, 2)
-        above(0, 3)
+        for t in range(PACK):
+            turn_r(0, t)
+            above(0, t)
         residual(1, 2)
         residual(1, 3)
         mm_low(2, 0)
         mm_low(2, 1)
 
         last = UNITS - 1
-        for unit in range(UNITS):
+        runs = {
+            3: ([(0, 0), (0, 1)], [(0, 2), (1, 0)]),
+            0: ([(1, 1), (1, 2)], [(0, 3), (1, 3)]),
+            1: ([(2, 0), (2, 1)], [(2, 2), (2, 3)]),
+            2: ([(3, 0), (3, 1)], [(3, 2), (3, 3)]),
+        }
+        for unit in range(last - 1):
             s, g = divmod(unit, GROUPS)
             nxt, far = unit + 1, unit + 2
-            more_u = s + 1 < STRIPS
+            so = (unit + 1) // GROUPS - 1
+            early, late = runs[g] if so >= 0 else ([], [])
             threshold(unit, 0)
             threshold(unit, 1)
-            if more_u and g == 1:
-                turn_u(s + 1, 2, 4)
-                copy_u(s + 1, 2, 4)
-            if nxt <= last:
-                turn_r(nxt, 0)
-                turn_r(nxt, 1)
-            if more_u and g == 0:
-                turn_u(s + 1, 0, 2)
-            if nxt <= last:
-                above(nxt, 0)
-                above(nxt, 1)
-            if more_u and g == 0:
-                copy_u(s + 1, 0, 2)
-            if far <= last:
-                residual(far, 0)
-                residual(far, 1)
-                mm_low(far, 2)
-                mm_low(far, 3)
-            if s > 0 and far <= last:
-                mm_out(s - 1, g, 0)
-                mm_out(s - 1, g, 1)
-            if unit == last - 1:
-                for gg in range(GROUPS):
-                    mm_out(s - 1, 3, gg)
-                store(s - 1, 3, nc.scalar.copy)
-                mm_out(s, 0, 0, "low")
-                mm_out(s, 1, 0, "low")
-            if unit == last:
-                weave_e(unit - 1, "act", 3 * P, W)
+            if unit == 1:
+                turn_u(1, 2, 4)
+                copy_u(1, 2, 4)
+            turn_r(nxt, 0)
+            turn_r(nxt, 1)
+            if unit == 0:
+                turn_u(1, 0, 2)
+            above(nxt, 0)
+            above(nxt, 1)
+            if unit == 0:
+                copy_u(1, 0, 2)
+            if unit == 3:
+                weave_f(3, "act", 0, C // 2)
+            residual(far, 0)
+            residual(far, 1)
+            mm_low(far, 2)
+            mm_low(far, 3)
+            for j, gg in early:
+                mm_out(so, j, gg)
             threshold(unit, 2)
-            if unit == last - 1:
-                quant_e(unit - 1, 0, W)
             threshold(unit, 3)
-            if 0 < unit and unit != last - 1:
+            if unit > 0:
                 quant_e(unit - 1, 0, W)
-            if more_u and g == 1:
-                quant_u(s + 1, 0, W)
+            if unit == 1:
+                quant_u(1, 0, W)
+            if g == 3 and s + 2 < STRIPS:
+                quant_u(s + 2, 0, W)
             if 1 <= unit <= GROUPS:
                 quant_f(unit - 1)
             difference(unit)
-            if unit < last - 1:
-                weave_e(unit, "pool", 0, W)
-            elif unit < last:
-                weave_e(unit, "pool", 0, 3 * P)
-            if nxt <= last:
-                turn_r(nxt, 2)
-                turn_r(nxt, 3)
-            if nxt <= last:
-                above(nxt, 2)
-                above(nxt, 3)
-            for gf, lo in {1: [(2, 0), (2, C // 2)], 2: [(3, 0)], 3: [(3, C // 2)]}.get(unit, []):
+            weave_e(unit, "pool", 0, W)
+            if g in (1, 2) and s + 2 < STRIPS:
+                turn_u(s + 2, 2 * g - 2, 2 * g)
+                copy_u(s + 2, 2 * g - 2, 2 * g)
+            turn_r(nxt, 2)
+            turn_r(nxt, 3)
+            above(nxt, 2)
+            above(nxt, 3)
+            for gf, lo in {1: [(2, 0)], 2: [(2, C // 2)], 3: [(3, C // 2)]}.get(unit, []):
                 weave_f(gf, "act", lo, lo + C // 2)
-            if s > 0 and far <= last:
-                mm_out(s - 1, g, 2)
-                mm_out(s - 1, g, 3)
-            if unit == last - 1:
-                mm_out(s, 0, 1)
-                mm_out(s, 1, 1)
-                for j in (2, 3):
-                    mm_out(s, j, 0)
-                    mm_out(s, j, 1)
-            if far <= last:
-                residual(far, 2)
-                residual(far, 3)
-            if far + 1 <= last:
+            for j, gg in late:
+                mm_out(so, j, gg)
+            residual(far, 2)
+            residual(far, 3)
+            if far < last:
                 mm_low(far + 1, 0)
                 mm_low(far + 1, 1)
-            if s > 0 and far <= last:
-                store(s - 1, g, nc.scalar.copy)
-            if far == last:
-                for gg in range(GROUPS):
-                    mm_out(s - 1, 2, gg)
-                store(s - 1, 2, nc.scalar.copy)
+            for j, gg in late:
+                if gg == GROUPS - 1:
+                    store(so, j, nc.scalar.copy)
 
         s = STRIPS - 1
+        for g in range(GROUPS):
+            mm_out(s - 1, 3, g)
+        for t in range(2):
+            threshold(last - 1, t)
+        for t in range(2):
+            turn_r(last, t)
+            above(last, t)
+        store(s - 1, 3, nc.scalar.copy)
+        mm_out(s, 0, 0, "low")
+        mm_out(s, 1, 0, "low")
+        mm_out(s, 2, 0)
+        threshold(last - 1, 2)
+        turn_r(last, 2)
+        above(last, 2)
+        quant_e(last - 2, 0, W)
+        threshold(last - 1, 3)
+        weave_e(last - 1, "pool", 0, 2 * P)
+        weave_e(last - 1, "act", 3 * P, W)
+        turn_r(last, 3)
+        above(last, 3)
+        weave_e(last - 1, "act", 2 * P, 3 * P)
+        mm_out(s, 3, 0)
+        for j in range(TILES):
+            mm_out(s, j, 1)
+        half = W // 2
+        for t in range(3):
+            threshold(last, t)
+        threshold(last, 3, 0, half)
         weave_e(last, "act", 0, P)
         weave_e(last, "act", P, 2 * P)
-        for j in range(TILES):
-            mm_out(s, j, 2)
+        quant_e(last - 1, 0, W)
+        threshold(last, 3, half, W)
+        weave_e(last, "act", 3 * P, W)
         weave_e(last, "dve", 2 * P, 3 * P)
-        quant_e(last, 0, P)
-        mm_out(s, 0, 3)
-        weave_e(last, "dve", 3 * P, W)
-        for j in (2, 1, 3):
+        for j in range(TILES):
             quant_e(last, j * P, (j + 1) * P)
-            mm_out(s, j, 3)
-        for j in (0, 2, 1, 3):
+        for j, g in ((0, 2), (1, 2), (0, 3), (2, 2), (1, 3), (3, 2), (2, 3), (3, 3)):
+            mm_out(s, j, g)
+        for j in range(TILES):
             store(s, j, nc.scalar.copy if j % 2 == 0 else nc.vector.tensor_copy)

from contextlib import ExitStack

import concourse.mybir as mybir
from concourse.masks import make_identity

M, K, N, C = 2048, 512, 2048, 512
FLOPS = 2 * M * K * N + 2 * M * N * C

F32 = mybir.dt.float32
BF16 = mybir.dt.bfloat16
I32 = mybir.dt.int32
U32 = mybir.dt.uint32
U8 = mybir.dt.uint8
E4M3 = mybir.dt.float8_e4m3fn_x4
E5M2 = mybir.dt.float8_e5m2_x4
E2M1 = mybir.dt.float4_e2m1fn_x4
ALU = mybir.AluOpType
ACT = mybir.ActivationFunctionType

P = 128
PACK = 4
W = 512
TILES = 4
STRIPS = M // W
GROUPS = N // W
UNITS = STRIPS * GROUPS
SCALAR_COLS = 288
FIRST_COLS = 0
EARLY_COLS = 272


def tile_robust_pca_sparse_step_s9_kernel(tc, u, v_words, v_scales, d, lam, f, out):
    nc = tc.nc
    with ExitStack() as ctx:
        sb = ctx.enter_context(tc.tile_pool(name="sb", bufs=1))
        ps = ctx.enter_context(tc.psum_pool(name="ps", bufs=1))
        ctx.enter_context(tc.manual_schedule())

        def sbuf(name, shape, dtype, bufs=1):
            return sb.tile(shape, dtype, name=name, tag=name, bufs=bufs, align_bytes=64)

        def bank(name, shape):
            return ps.tile(shape, F32, name=name, tag=name, bufs={"low": 2, "res": 4, "acc": 2}[name])

        u_rows = u.rearrange("(s p j) k -> s p j k", p=P, j=TILES)
        d_rows = d.rearrange("(s p j) n -> s p j n", p=P, j=TILES)
        out_rows = out.rearrange("(s p j) c -> s p j c", p=P, j=TILES)
        f_rows = f.rearrange("(g q t r) c -> g r q t c", q=16, t=PACK, r=8)

        u_raw, d_raw, f_raw = {}, {}, {}

        def load_u(s, lo, hi):
            piece = sbuf("u_raw", [P, hi - lo, K], BF16, bufs=2 * STRIPS)
            nc.sync.dma_start(out=piece[:], in_=u_rows[s, :, lo:hi, :])
            for j in range(lo, hi):
                u_raw[s, j] = piece[:, j - lo, :]

        def load_d(unit):
            s, g = divmod(unit, GROUPS)
            piece = sbuf("d_raw", [P, TILES, W], BF16, bufs=UNITS)
            nc.sync.dma_start(out=piece[:], in_=d_rows[s, :, :, g * W : (g + 1) * W])
            for j in range(TILES):
                d_raw[unit, j] = piece[:, j, :]

        def load_d_first(lo):
            piece = sbuf("d_raw", [P, 2, 2 * W], BF16, bufs=UNITS)
            nc.sync.dma_start(out=piece[:], in_=d_rows[0, :, lo : lo + 2, 0 : 2 * W])
            for j in (lo, lo + 1):
                for g in range(2):
                    d_raw[g, j] = piece[:, j - lo, g * W : (g + 1) * W]

        def load_f(g, lo=0, hi=8):
            if lo == 0:
                f_raw[g] = sbuf("f_raw", [P, PACK, C], BF16, bufs=GROUPS)
            for r in range(lo, hi):
                nc.sync.dma_start(out=f_raw[g][r:P:8, :, :], in_=f_rows[g, r])

        v_plane = sbuf("v_plane", [P, N], U8)
        nc.vector.memset(v_plane[:].bitcast(I32), 0)
        ident = sbuf("ident", [P, P], F32)
        make_identity(nc, ident[:])
        lam_f32 = sbuf("lam_f32", [P, W], F32)
        nc.gpsimd.memset(lam_f32[:], 0.0)

        lam_rows = sbuf("lam_rows", [P, W], BF16)
        v_codes = {}

        def load_v(g):
            piece = sbuf("v_codes", [P, 4 * W], U8, bufs=2)
            nc.sync.dma_start(out=piece[:].bitcast(I32), in_=v_words[0][:, 2 * W * g : 2 * W * (g + 2)].bitcast(I32))
            v_codes[g] = piece[:, 0 : 2 * W]
            v_codes[g + 1] = piece[:, 2 * W : 4 * W]

        load_u(0, 0, 2)
        load_v(0)
        for quad in range(4):
            nc.sync.dma_start(
                out=v_plane[32 * quad : 32 * quad + 4, :].bitcast(I32),
                in_=v_scales[0][4 * quad : 4 * quad + 4, :].bitcast(I32),
            )
        load_d_first(0)
        load_u(0, 2, 4)
        load_d_first(2)
        nc.sync.dma_start(out=lam_rows[0:GROUPS, :], in_=lam.rearrange("(g n) -> g n", g=GROUPS))
        load_f(0)
        load_v(2)
        load_f(1, 0, 4)
        load_d(2)
        load_f(1, 4, 8)
        load_u(1, 0, 2)
        load_u(1, 2, 4)
        load_d(3)
        load_f(2)
        load_u(2, 0, 2)
        load_d(4)
        load_u(2, 2, 4)
        load_f(3)
        load_d(5)
        load_u(3, 0, 2)
        load_u(3, 2, 4)
        for unit in range(6, UNITS):
            load_d(unit)

        u_turned, u_words, u_codes, u_scale = {}, {}, {}, {}

        def turn_u(s, lo, hi):
            u_turned[s, lo] = bank("acc", [P, hi - lo, 2, P])
            for j in range(lo, hi):
                words = u_raw[s, j].bitcast(F32)
                for w in range(2):
                    nc.tensor.transpose(u_turned[s, lo][:, j - lo, w, :], words[:, w : K // 2 : 2], ident[:])

        def copy_u(s, lo, hi):
            if lo == 0:
                u_words[s] = sbuf("u_words", [P, PACK * W], BF16, bufs=2)
            part = u_words[s][:, lo * PACK * P : hi * PACK * P].bitcast(F32)
            nc.scalar.copy(
                out=part.rearrange("p (j m w) -> p j m w", m=P, w=2),
                in_=u_turned[s, lo][:].rearrange("p j w m -> p j m w"),
            )

        def quant_u(s, lo, hi):
            if lo == 0:
                u_codes[s] = sbuf("u_codes", [P, W], U32, bufs=STRIPS)
                u_scale[s] = sbuf("u_scale", [P, W], U8, bufs=STRIPS)
            nc.vector.quantize_mx(
                out=u_codes[s][:, lo:hi].bitcast(E4M3),
                scales=u_scale[s][:, lo:hi],
                in_=u_words[s][:, PACK * lo : PACK * hi],
            )

        f_words, f_codes, f_scale = {}, {}, {}

        def weave(engine, dst, src):
            if engine == "pool":
                o = dst.rearrange("p (c t) -> p c t", t=PACK)
                i = src.rearrange("p t c -> p c t")
                nc.gpsimd.tensor_scalar(o, i, 1.0, 0.0, ALU.mult, ALU.add)
            else:
                o = dst.rearrange("p (c i t) -> p c t i", i=4, t=PACK)
                i = src.rearrange("p t (c i) -> p c t i", i=4)
                if engine == "act":
                    nc.scalar.copy(out=o, in_=i)
                else:
                    nc.vector.tensor_copy(out=o, in_=i)

        def weave_f(g, engine, lo, hi):
            if lo == 0:
                f_words[g] = sbuf("f_words", [P, PACK * C], BF16, bufs=GROUPS)
            weave(engine, f_words[g][:, PACK * lo : PACK * hi], f_raw[g][:, :, lo:hi])

        def quant_f(g):
            f_codes[g] = sbuf("f_codes", [P, C], U32, bufs=GROUPS)
            f_scale[g] = sbuf("f_scale", [P, C], U8, bufs=GROUPS)
            nc.vector.quantize_mx(out=f_codes[g][:].bitcast(E4M3), scales=f_scale[g][:], in_=f_words[g][:])

        lower = {}
        low, resid, turned, upper, sparse, woven, e_codes, e_scale, acc = {}, {}, {}, {}, {}, {}, {}, {}, {}

        def mm_low(unit, j):
            s, g = divmod(unit, GROUPS)
            low[unit, j] = bank("low", [P, W])
            cols = slice(j * P, (j + 1) * P)
            nc.tensor.matmul_mx(
                out=low[unit, j][:],
                lhsT=u_codes[s][:, cols].bitcast(E4M3),
                lhsT_scale=u_scale[s][:, cols],
                rhs=v_codes[g].bitcast(E2M1),
                rhs_scale=v_plane[:, g * W : (g + 1) * W],
                start=True,
                stop=True,
            )

        def residual(unit, j):
            resid[unit, j] = sbuf("resid", [P, W], F32, bufs=2 * TILES)
            nc.vector.tensor_tensor(
                out=resid[unit, j][:].rearrange("p (t q r) -> p q t r", t=PACK, r=8),
                in0=d_raw[unit, j].rearrange("p (q t r) -> p q t r", t=PACK, r=8),
                in1=low[unit, j][:].rearrange("p (q t r) -> p q t r", t=PACK, r=8),
                op=ALU.subtract,
            )

        def turn_r(unit, t):
            turned[unit, t] = bank("res", [P, W])
            for j in range(TILES):
                nc.tensor.transpose(
                    turned[unit, t][:, j * P : (j + 1) * P], resid[unit, j][:, t * P : (t + 1) * P], ident[:]
                )

        def split(unit):
            return FIRST_COLS if unit == 0 else 0 if unit >= UNITS - 2 else EARLY_COLS if 2 <= unit <= 4 else SCALAR_COLS

        def above(unit, t):
            g, c = unit % GROUPS, split(unit)
            if t == 0:
                upper[unit] = sbuf("upper", [P, PACK, W], BF16, bufs=2)
                if c:
                    lower[unit] = sbuf("lower", [P, PACK, c], BF16, bufs=2)
            bias = lam_neg[:, t, g : g + 1]
            nc.scalar.activation(out=upper[unit][:, t, :], in_=turned[unit, t][:], func=ACT.Relu, bias=bias, scale=1.0)
            if c:
                nc.scalar.activation(
                    out=lower[unit][:, t, :], in_=turned[unit, t][:, 0:c], func=ACT.Relu, bias=bias, scale=-1.0
                )

        def threshold(unit, t, lo=None, hi=W):
            g = unit % GROUPS
            c = split(unit) if lo is None else lo
            if unit not in sparse:
                sparse[unit] = sbuf("sparse", [P, PACK, W], BF16, bufs=2)
            nc.vector.scalar_tensor_tensor(
                out=sparse[unit][:, t, c:hi],
                in0=turned[unit, t][:, c:hi],
                scalar=lam_pos[:, t, g : g + 1],
                in1=upper[unit][:, t, c:hi],
                op0=ALU.add,
                op1=ALU.min,
            )

        def woven_cols(unit, lo, hi):
            if unit not in woven:
                woven[unit] = sbuf("woven", [P, PACK * W], BF16, bufs=3)
            return woven[unit][:, PACK * lo : PACK * hi]

        def weave_e(unit, engine, lo, hi):
            weave(engine, woven_cols(unit, lo, hi), sparse[unit][:, :, lo:hi])

        def difference(unit):
            c = split(unit)
            if c:
                nc.vector.tensor_tensor(
                    out=sparse[unit][:, :, 0:c], in0=upper[unit][:, :, 0:c], in1=lower[unit][:], op=ALU.subtract
                )

        def quant_e(unit, lo, hi):
            if unit not in e_codes:
                e_codes[unit] = sbuf("e_codes", [P, W], U32, bufs=2 * GROUPS)
                e_scale[unit] = sbuf("e_scale", [P, W], U8, bufs=2 * GROUPS)
            nc.vector.quantize_mx(
                out=e_codes[unit][:, lo:hi].bitcast(E5M2),
                scales=e_scale[unit][:, lo:hi],
                in_=woven[unit][:, PACK * lo : PACK * hi],
            )

        def mm_out(s, j, g, name="acc"):
            if g == 0:
                acc[s, j] = bank(name, [P, C])
            unit = s * GROUPS + g
            cols = slice(j * P, (j + 1) * P)
            nc.tensor.matmul_mx(
                out=acc[s, j][:],
                lhsT=e_codes[unit][:, cols].bitcast(E5M2),
                lhsT_scale=e_scale[unit][:, cols],
                rhs=f_codes[g][:].bitcast(E4M3),
                rhs_scale=f_scale[g][:],
                start=(g == 0),
                stop=(g == GROUPS - 1),
            )

        def store(s, j, copy):
            result = sbuf("result", [P, C], F32, bufs=4)
            copy(out=result[:], in_=acc[s, j][:])
            nc.sync.dma_start(out=out_rows[s, :, j, :], in_=result[:])

        def first_u(j):
            turn_u(0, j, j + 1)
            copy_u(0, j, j + 1)

        first_u(0)
        first_u(1)
        quant_u(0, 0, P)
        mm_low(0, 0)
        mm_low(1, 0)
        quant_u(0, P, 2 * P)
        first_u(2)
        first_u(3)
        residual(0, 0)
        mm_low(0, 1)
        residual(1, 0)
        mm_low(1, 1)
        quant_u(0, 2 * P, W)
        nc.vector.tensor_copy(
            out=lam_f32[0:GROUPS, :].rearrange("g (t q r) -> g q t r", t=PACK, r=8),
            in_=lam_rows[0:GROUPS, :].rearrange("g (q t r) -> g q t r", t=PACK, r=8),
        )
        residual(0, 1)
        mm_low(0, 2)
        residual(1, 1)
        mm_low(0, 3)
        lam_turned = bank("acc", [P, PACK, P])
        lam_pos = sbuf("lam_pos", [P, PACK, GROUPS], F32)
        lam_neg = sbuf("lam_neg", [P, PACK, GROUPS], F32)
        for t in range(PACK):
            nc.tensor.transpose(lam_turned[:, t, :], lam_f32[:, t * P : (t + 1) * P], ident[:])
        nc.scalar.activation(out=lam_neg[:], in_=lam_turned[:, :, 0:GROUPS], func=ACT.Copy, scale=-1.0)
        nc.scalar.copy(out=lam_pos[:], in_=lam_turned[:, :, 0:GROUPS])
        residual(0, 2)
        mm_low(1, 2)
        residual(0, 3)
        mm_low(1, 3)
        weave_f(0, "pool", 0, C)
        weave_f(1, "pool", 0, C)
        for t in range(PACK):
            turn_r(0, t)
            above(0, t)
        residual(1, 2)
        residual(1, 3)
        mm_low(2, 0)
        mm_low(2, 1)

        last = UNITS - 1
        runs = {
            3: ([(0, 0), (0, 1)], [(0, 2), (1, 0)]),
            0: ([(1, 1), (1, 2)], [(0, 3), (1, 3)]),
            1: ([(2, 0), (2, 1)], [(2, 2), (2, 3)]),
            2: ([(3, 0), (3, 1)], [(3, 2), (3, 3)]),
        }
        for unit in range(last - 1):
            s, g = divmod(unit, GROUPS)
            nxt, far = unit + 1, unit + 2
            so = (unit + 1) // GROUPS - 1
            early, late = runs[g] if so >= 0 else ([], [])
            threshold(unit, 0)
            threshold(unit, 1)
            if unit == 1:
                turn_u(1, 2, 4)
                copy_u(1, 2, 4)
            turn_r(nxt, 0)
            turn_r(nxt, 1)
            if unit == 0:
                turn_u(1, 0, 2)
            above(nxt, 0)
            above(nxt, 1)
            if unit == 0:
                copy_u(1, 0, 2)
            if unit == 3:
                weave_f(3, "act", 0, C // 2)
            residual(far, 0)
            residual(far, 1)
            mm_low(far, 2)
            mm_low(far, 3)
            for j, gg in early:
                mm_out(so, j, gg)
            threshold(unit, 2)
            threshold(unit, 3)
            if unit > 0:
                quant_e(unit - 1, 0, W)
            if unit == 1:
                quant_u(1, 0, W)
            if g == 3 and s + 2 < STRIPS:
                quant_u(s + 2, 0, W)
            if 1 <= unit <= GROUPS:
                quant_f(unit - 1)
            difference(unit)
            weave_e(unit, "pool", 0, W)
            if g in (1, 2) and s + 2 < STRIPS:
                turn_u(s + 2, 2 * g - 2, 2 * g)
                copy_u(s + 2, 2 * g - 2, 2 * g)
            turn_r(nxt, 2)
            turn_r(nxt, 3)
            above(nxt, 2)
            above(nxt, 3)
            for gf, lo in {1: [(2, 0)], 2: [(2, C // 2)], 3: [(3, C // 2)]}.get(unit, []):
                weave_f(gf, "act", lo, lo + C // 2)
            for j, gg in late:
                mm_out(so, j, gg)
            residual(far, 2)
            residual(far, 3)
            if far < last:
                mm_low(far + 1, 0)
                mm_low(far + 1, 1)
            for j, gg in late:
                if gg == GROUPS - 1:
                    store(so, j, nc.scalar.copy)

        s = STRIPS - 1
        for g in range(GROUPS):
            mm_out(s - 1, 3, g)
        for t in range(2):
            threshold(last - 1, t)
        for t in range(2):
            turn_r(last, t)
            above(last, t)
        store(s - 1, 3, nc.scalar.copy)
        mm_out(s, 0, 0, "low")
        mm_out(s, 1, 0, "low")
        mm_out(s, 2, 0)
        threshold(last - 1, 2)
        turn_r(last, 2)
        above(last, 2)
        quant_e(last - 2, 0, W)
        threshold(last - 1, 3)
        weave_e(last - 1, "pool", 0, 2 * P)
        weave_e(last - 1, "act", 3 * P, W)
        turn_r(last, 3)
        above(last, 3)
        weave_e(last - 1, "act", 2 * P, 3 * P)
        mm_out(s, 3, 0)
        for j in range(TILES):
            mm_out(s, j, 1)
        half = W // 2
        for t in range(3):
            threshold(last, t)
        threshold(last, 3, 0, half)
        weave_e(last, "act", 0, P)
        weave_e(last, "act", P, 2 * P)
        quant_e(last - 1, 0, W)
        threshold(last, 3, half, W)
        weave_e(last, "act", 3 * P, W)
        weave_e(last, "dve", 2 * P, 3 * P)
        for j in range(TILES):
            quant_e(last, j * P, (j + 1) * P)
        for j, g in ((0, 2), (1, 2), (0, 3), (2, 2), (1, 3), (3, 2), (2, 3), (3, 3)):
            mm_out(s, j, g)
        for j in range(TILES):
            store(s, j, nc.scalar.copy if j % 2 == 0 else nc.vector.tensor_copy)
